import numpy as np
import ml_dtypes


def mxq(x, axis, fmt="e4m3"):
    dtype, down = {"e4m3": (ml_dtypes.float8_e4m3fn, 7), "e5m2": (ml_dtypes.float8_e5m2, 14)}[fmt]
    v = np.moveaxis(np.asarray(x, np.float32).astype(ml_dtypes.bfloat16).astype(np.float64), axis, -1)
    blocks = v.reshape(v.shape[:-1] + (-1, 32))
    amax = np.abs(blocks).max(-1, keepdims=True)
    byte = np.maximum(np.where(amax > 0, np.frexp(amax)[1] - 1 + 127, 0) - down, 1)
    scale = np.exp2(byte - 127.0)
    codes = (blocks / scale).astype(np.float32).astype(dtype).astype(np.float64)
    return np.moveaxis((codes * scale).reshape(v.shape), -1, axis)


WIDE = False


def mx_kscale(k):
    if not WIDE:
        return np.ones(k)
    levels = np.array([10, -10, 5, -5, 0])
    if k % 512:
        return np.exp2(np.random.permutation(np.resize(levels, k // 32))).repeat(32)
    a = np.empty((k // 512, 16))
    for p in range(k // 512):
        a[p, :8] = np.random.permutation(np.resize(levels, 8))
        for g in range(8):
            far = levels[np.abs(levels - a[p, g]) >= 10]
            a[p, g + 8] = far[np.random.randint(len(far))]
    return np.exp2(a.ravel()).repeat(32)


def f64(x):
    return np.asarray(x).astype(np.float64)


def striped(idx):
    return np.tile(idx.reshape(-1, 16).T, (8, 1)).astype(np.uint16)


def unstriped(offs):
    return offs[:16].T.reshape(-1).astype(np.int64)


E2M1 = np.array([0.0, 0.5, 1.0, 1.5, 2.0, 3.0, 4.0, 6.0, -0.0, -0.5, -1.0, -1.5, -2.0, -3.0, -4.0, -6.0])


def pack_weight(w, fmt):
    k, n = w.shape
    w = f64(np.asarray(w, np.float32).astype(ml_dtypes.bfloat16)).reshape(k // 32, 32, n)
    amax = np.abs(w).max(1)
    if fmt == "e4m3":
        byte = np.frexp(amax)[1] - 1 + 127 - 7
    else:
        mant, ex = np.frexp(amax / 6.0)
        byte = np.where(mant > 0.5, ex, ex - 1) + 127
    byte = np.clip(np.where(amax > 0, byte, 1), 1, 254)
    scaled = (w * np.exp2(127.0 - byte)[:, None, :]).reshape(k, n).astype(np.float32)
    by_word = np.ascontiguousarray(scaled.reshape(k // 512, 128, 4, n).transpose(0, 1, 3, 2))
    if fmt == "e4m3":
        words = by_word.astype(ml_dtypes.float8_e4m3fn).view(np.uint8)
    else:
        c = by_word.astype(ml_dtypes.float4_e2m1fn).view(np.uint8) & 0xF
        words = (c[..., 0::2] | (c[..., 1::2] << 4)).reshape(k // 512, 128, 2 * n)
    return np.ascontiguousarray(words), np.ascontiguousarray(byte.astype(np.uint8).reshape(k // 512, 16, n))


def unpack_weight(words, scales, fmt):
    g, _, n = scales.shape
    words = np.ascontiguousarray(words).reshape(g, 128, n, -1)
    if fmt == "e4m3":
        vals = words.view(ml_dtypes.float8_e4m3fn).astype(np.float64)
    else:
        nib = np.empty((g, 128, n, 4), np.uint8)
        nib[..., 0::2] = words & 0xF
        nib[..., 1::2] = words >> 4
        vals = E2M1[nib]
    vals = vals * np.repeat(np.exp2(scales.astype(np.float64) - 127.0), 8, axis=1)[..., None]
    return vals.transpose(0, 1, 3, 2).reshape(g * 512, n)


def relu(v):
    return np.maximum(v, 0.0)


K, T, E, H, N = 2560, 512, 2, 512, 256
COUNTS = (128, 384)
STARTS = np.cumsum((0,) + COUNTS)


def by_expert(wq, xq):
    return np.concatenate([wq[e].T @ xq[:, STARTS[e]:STARTS[e + 1]] for e in range(E)], axis=1)


def setup_inputs():
    n = np.random.standard_normal
    s = mx_kscale(K)[:, None]
    u = mx_kscale(H)
    expert = np.random.permutation(np.repeat(np.arange(E), COUNTS))
    slot_token = np.argsort(expert, kind="stable")
    w1 = [pack_weight(m, "e2m1") for m in n((E, K, H)) / np.sqrt(K) / s[None]]
    w3 = [pack_weight(m, "e2m1") for m in n((E, K, H)) / np.sqrt(K) / s[None] * u[None, None, :]]
    w2 = [pack_weight(m, "e2m1") for m in n((E, H, N)) / np.sqrt(H) / u[None, :, None]]
    return {
        "xT": (n((K, T)) * s).astype(np.float32),
        "w1_words": np.stack([m[0] for m in w1]),
        "w1_scales": np.stack([m[1] for m in w1]),
        "w3_words": np.stack([m[0] for m in w3]),
        "w3_scales": np.stack([m[1] for m in w3]),
        "w2_words": np.stack([m[0] for m in w2]),
        "w2_scales": np.stack([m[1] for m in w2]),
        "gate": np.tile(np.random.uniform(0.2, 1.0, T), (N, 1)).astype(np.float32),
        "offs": striped(slot_token),
    }


def reference(xT, w1_words, w1_scales, w3_words, w3_scales, w2_words, w2_scales, gate, offs):
    idx = unstriped(offs)
    w1 = np.stack([unpack_weight(w1_words[e], w1_scales[e], "e2m1") for e in range(E)])
    w3 = np.stack([unpack_weight(w3_words[e], w3_scales[e], "e2m1") for e in range(E)])
    w2 = np.stack([unpack_weight(w2_words[e], w2_scales[e], "e2m1") for e in range(E)])
    xq = mxq(f64(xT)[:, idx], 0, "e4m3")
    h = relu(by_expert(w1, xq))
    h = h * by_expert(w3, xq)
    y = by_expert(w2, mxq(h, 0, "e4m3"))
    out = np.zeros((N, T))
    out[:, idx] = f64(gate) * y
    return out

@@ -1,0 +1,197 @@
+from contextlib import ExitStack
+
+import concourse.mybir as mybir
+from concourse.masks import make_identity
+
+FLOPS = 2818572288
+
+F32 = mybir.dt.float32
+BF16 = mybir.dt.bfloat16
+I32 = mybir.dt.int32
+U32 = mybir.dt.uint32
+U16 = mybir.dt.uint16
+U8 = mybir.dt.uint8
+E4M3 = mybir.dt.float8_e4m3fn_x4
+E2M1 = mybir.dt.float4_e2m1fn_x4
+COPY = mybir.ActivationFunctionType.Copy
+RELU = mybir.ActivationFunctionType.Relu
+MULT = mybir.AluOpType.mult
+
+P = 128
+T = 512
+E = 2
+H = 512
+N = 256
+PASSES = 5
+TILES = 4
+TILE_EXPERT = (0, 1, 1, 1)
+VECTOR_COLS = (256, 128, 128, 128, 256)
+LIST_CUTS = ((0, 128), (128, 512))
+LAST_CUTS = ((0, 128), (128, 256), (256, 384), (384, 512))
+
+
+def interleave(ap_in, ap_out):
+    return (
+        ap_out.rearrange("p (c i) t -> p c t i", i=4),
+        ap_in.rearrange("p t (c i) -> p c t i", i=4),
+    )
+
+
+def tile_moe_rag_glu_relu_kernel(
+    tc, xT, w1_words, w1_scales, w3_words, w3_scales, w2_words, w2_scales, gate, offs, out
+):
+    nc = tc.nc
+    with ExitStack() as ctx:
+        held = ctx.enter_context(tc.tile_pool(name="held", bufs=1))
+        psum = ctx.enter_context(tc.psum_pool(name="psum", bufs=1))
+
+        offsets = held.tile([P, T // 16], U16, name="offsets")
+        x_raw = [held.tile([P, 4, T], F32, name=f"x_raw{s}") for s in range(PASSES)]
+        x_bf = [held.tile([P, T, 4], BF16, name=f"x_bf{s}", align_bytes=64) for s in range(PASSES)]
+        tok_codes = [held.tile([P, T], U32, name=f"tok_codes{s}", align_bytes=64) for s in range(PASSES)]
+        tok_scales = [held.tile([P, T], U8, name=f"tok_scales{s}", align_bytes=64) for s in range(PASSES)]
+        slot_codes = [held.tile([P, T], U32, name=f"slot_codes{s}", align_bytes=64) for s in range(PASSES)]
+        slot_scales = [held.tile([P, T], U8, name=f"slot_scales{s}", align_bytes=64) for s in range(PASSES)]
+        words = [
+            [held.tile([P, E, 2 * H], U8, name=f"words{w}_{s}", align_bytes=64) for w in range(2)]
+            for s in range(PASSES)
+        ]
+        planes = [held.tile([P, E * PASSES, H], U8, name=f"planes{w}", align_bytes=64) for w in range(2)]
+        w2_codes = held.tile([P, E, 2 * N], U8, name="w2_codes", align_bytes=64)
+        w2_plane = held.tile([P, E, N], U8, name="w2_plane", align_bytes=64)
+        gates = held.tile([P, 2, T], F32, name="gates")
+        identity = held.tile([P, P], F32, name="identity")
+        y_slots = held.tile([P, 2, T], F32, name="y_slots")
+        y_tokens = [held.tile([P, T], F32, name=f"y_tokens{t}") for t in range(2)]
+        banks = [[psum.tile([P, H], F32, name=f"bank{w}_{m}", tag=f"bank{w}_{m}") for w in range(2)] for m in range(TILES)]
+
+        w_dram = (w1_words, w3_words)
+
+        def load_x(s):
+            nc.sync.dma_start(
+                out=x_raw[s][:], in_=xT[4 * P * s : 4 * P * (s + 1), :].rearrange("(p j) w -> p j w", j=4)
+            )
+
+        def load_w(s, experts):
+            for w in range(2):
+                nc.sync.dma_start(
+                    out=words[s][w][:, experts, :].bitcast(I32),
+                    in_=w_dram[w][experts, s].rearrange("e p b -> p e b").bitcast(I32),
+                )
+
+        both = slice(0, E)
+        load_x(0)
+        nc.sync.dma_start(offsets[:], offs)
+        load_x(1)
+        load_w(0, both)
+        load_x(2)
+        load_w(1, both)
+        load_x(3)
+        load_w(2, both)
+        load_x(4)
+        load_w(3, both)
+        nc.sync.dma_start(
+            out=w2_codes[:].bitcast(I32), in_=w2_words[:, 0].rearrange("e p b -> p e b").bitcast(I32)
+        )
+        load_w(4, slice(0, 1))
+        load_w(4, slice(1, 2))
+        nc.sync.dma_start(out=gates[:], in_=gate.rearrange("(t p) s -> p t s", p=P))
+
+        for w in range(2):
+            nc.vector.memset(planes[w][:].bitcast(I32), 0)
+        for s in range(PASSES):
+            nc.vector.memset(tok_scales[s][:].bitcast(I32), 0)
+        nc.vector.memset(w2_plane[:].bitcast(I32), 0)
+        for plane, dram in ((planes[0], w1_scales), (planes[1], w3_scales), (w2_plane, w2_scales)):
+            by_row = dram.rearrange("e s (q r) i -> r q (e s) i", r=4)
+            for r in range(4):
+                nc.gpsimd.dma_start(out=plane[r:P:32].bitcast(I32), in_=by_row[r].bitcast(I32))
+        make_identity(nc, identity[:])
+
+        def tokens(s):
+            cut = T - VECTOR_COLS[s]
+            dst, src = interleave(x_raw[s][:, :, :cut], x_bf[s][:, :cut, :])
+            nc.scalar.activation(dst, src, COPY)
+            dst, src = interleave(x_raw[s][:, :, cut:], x_bf[s][:, cut:, :])
+            nc.vector.tensor_copy(dst, src)
+            nc.vector.quantize_mx(
+                out=tok_codes[s][:].bitcast(E4M3),
+                scales=tok_scales[s][:],
+                in_=x_bf[s][:].rearrange("p w j -> p (w j)"),
+            )
+
+        def gather(s, cuts):
+            for a, b in cuts:
+                picked = offsets[:, a // 16 : b // 16]
+                nc.vector.tensor_copy(slot_codes[s][:, a:b], tok_codes[s][:].indirect(picked))
+                nc.vector.tensor_copy(slot_scales[s][:, a:b], tok_scales[s][:].indirect(picked))
+
+        def multiply(s, m):
+            e = TILE_EXPERT[m]
+            cols = slice(P * m, P * (m + 1))
+            for w in range(2):
+                nc.tensor.matmul_mx(
+                    out=banks[m][w][:],
+                    lhsT=slot_codes[s][:, cols].bitcast(E4M3),
+                    lhsT_scale=slot_scales[s][:, cols],
+                    rhs=words[s][w][:, e, :].bitcast(E2M1),
+                    rhs_scale=planes[w][:, e * PASSES + s, :],
+                    start=(s == 0),
+                    stop=(s == PASSES - 1),
+                )
+
+        for s in range(PASSES):
+            tokens(s)
+            gather(s, LIST_CUTS if s < PASSES - 1 else LAST_CUTS)
+            for m in range(TILES):
+                multiply(s, m)
+
+        for m in range(TILES):
+            e = TILE_EXPERT[m]
+            cols = slice(P * m, P * (m + 1))
+            a_pos = held.tile([P, H], F32, name=f"a_pos{m}")
+            nc.scalar.activation(a_pos[:], banks[m][0][:], RELU)
+            h = held.tile([P, 2, P, 2], BF16, name=f"h{m}", align_bytes=64)
+            nc.vector.tensor_tensor(
+                h[:],
+                banks[m][1][:].rearrange("p (q u v) -> p u q v", u=2, v=2),
+                a_pos[:].rearrange("p (q u v) -> p u q v", u=2, v=2),
+                MULT,
+            )
+            turned = psum.tile([P, 2, P], F32, name=f"turned{m}", tag=f"bank0_{m}")
+            pairs = h[:].rearrange("p u q v -> p (u q v)").bitcast(F32)
+            for u in range(2):
+                nc.tensor.transpose(turned[:, u, :], pairs[:, P * u : P * (u + 1)], identity[:])
+            h_in = held.tile([P, P, 4], BF16, name=f"h_in{m}", align_bytes=64)
+            nc.scalar.copy(
+                h_in[:].rearrange("p c d -> p (c d)").bitcast(F32).rearrange("p (c u) -> p c u", u=2),
+                turned[:].rearrange("p u c -> p c u"),
+            )
+            h_codes = held.tile([P, P], U32, name=f"h_codes{m}", align_bytes=64)
+            h_scales = held.tile([P, P], U8, name=f"h_scales{m}", align_bytes=64)
+            nc.vector.quantize_mx(
+                out=h_codes[:].bitcast(E4M3), scales=h_scales[:], in_=h_in[:].rearrange("p c d -> p (c d)")
+            )
+            y = psum.tile([P, 2, P], F32, name=f"y{m}", tag=f"bank1_{m}")
+            for t in range(2):
+                nc.tensor.matmul_mx(
+                    out=y[:, t, :],
+                    lhsT=w2_codes[:, e, 2 * P * t : 2 * P * (t + 1)].bitcast(E2M1),
+                    lhsT_scale=w2_plane[:, e, P * t : P * (t + 1)],
+                    rhs=h_codes[:].bitcast(E4M3),
+                    rhs_scale=h_scales[:],
+                    start=True,
+                    stop=True,
+                )
+            nc.scalar.copy(y_slots[:, :, cols], y[:])
+            if m > 0:
+                first = 0 if m == 1 else P * m
+                for t in range(2):
+                    nc.vector.tensor_tensor(
+                        y_tokens[t][:].indirect(offsets[:, first // 16 : P * (m + 1) // 16]),
+                        y_slots[:, t, first : P * (m + 1)],
+                        gates[:, t, first : P * (m + 1)],
+                        MULT,
+                    )
+        for t in range(2):
+            nc.sync.dma_start(out=out[P * t : P * (t + 1), :], in_=y_tokens[t][:])

@@ -25,9 +25,9 @@ N = 256
 PASSES = 5
 TILES = 4
 TILE_EXPERT = (0, 1, 1, 1)
-VECTOR_COLS = (256, 128, 128, 128, 256)
+VECTOR_COLS = (256, 0, 0, 0, 128)
 LIST_CUTS = ((0, 128), (128, 512))
-LAST_CUTS = ((0, 128), (128, 256), (256, 384), (384, 512))
+LAST_CUTS = ((0, 256), (256, 512))
 
 
 def interleave(ap_in, ap_out):
@@ -43,12 +43,11 @@ def tile_moe_rag_glu_relu_kernel(
     nc = tc.nc
     with ExitStack() as ctx:
         held = ctx.enter_context(tc.tile_pool(name="held", bufs=1))
+        ring = ctx.enter_context(tc.tile_pool(name="ring", bufs=2))
         psum = ctx.enter_context(tc.psum_pool(name="psum", bufs=1))
 
         offsets = held.tile([P, T // 16], U16, name="offsets")
-        x_raw = [held.tile([P, 4, T], F32, name=f"x_raw{s}") for s in range(PASSES)]
-        x_bf = [held.tile([P, T, 4], BF16, name=f"x_bf{s}", align_bytes=64) for s in range(PASSES)]
-        tok_codes = [held.tile([P, T], U32, name=f"tok_codes{s}", align_bytes=64) for s in range(PASSES)]
+        x_raw = {}
         tok_scales = [held.tile([P, T], U8, name=f"tok_scales{s}", align_bytes=64) for s in range(PASSES)]
         slot_codes = [held.tile([P, T], U32, name=f"slot_codes{s}", align_bytes=64) for s in range(PASSES)]
         slot_scales = [held.tile([P, T], U8, name=f"slot_scales{s}", align_bytes=64) for s in range(PASSES)]
@@ -67,9 +66,12 @@ def tile_moe_rag_glu_relu_kernel(
 
         w_dram = (w1_words, w3_words)
 
-        def load_x(s):
+        def load_x(s, cols=slice(0, T)):
+            if s not in x_raw:
+                x_raw[s] = ring.tile([P, 4, T], F32, name="x_raw", bufs=3)
             nc.sync.dma_start(
-                out=x_raw[s][:], in_=xT[4 * P * s : 4 * P * (s + 1), :].rearrange("(p j) w -> p j w", j=4)
+                out=x_raw[s][:, :, cols],
+                in_=xT[4 * P * s : 4 * P * (s + 1), cols].rearrange("(p j) w -> p j w", j=4),
             )
 
         def load_w(s, experts):
@@ -79,10 +81,17 @@ def tile_moe_rag_glu_relu_kernel(
                     in_=w_dram[w][experts, s].rearrange("e p b -> p e b").bitcast(I32),
                 )
 
+        nc.vector.memset(planes[0][:].bitcast(I32), 0)
+        nc.gpsimd.memset(planes[1][:].bitcast(I32), 0)
         both = slice(0, E)
-        load_x(0)
+        load_x(0, slice(0, 256))
+        load_x(0, slice(256, 512))
         nc.sync.dma_start(offsets[:], offs)
         load_x(1)
+        for plane, dram in ((planes[0], w1_scales), (planes[1], w3_scales)):
+            by_row = dram.rearrange("e s (q r) i -> r q (e s) i", r=4)
+            for r in range(4):
+                nc.sync.dma_start(out=plane[r:P:32].bitcast(I32), in_=by_row[r].bitcast(I32))
         load_w(0, both)
         load_x(2)
         load_w(1, both)
@@ -97,27 +106,29 @@ def tile_moe_rag_glu_relu_kernel(
         load_w(4, slice(1, 2))
         nc.sync.dma_start(out=gates[:], in_=gate.rearrange("(t p) s -> p t s", p=P))
 
-        for w in range(2):
-            nc.vector.memset(planes[w][:].bitcast(I32), 0)
         for s in range(PASSES):
             nc.vector.memset(tok_scales[s][:].bitcast(I32), 0)
         nc.vector.memset(w2_plane[:].bitcast(I32), 0)
-        for plane, dram in ((planes[0], w1_scales), (planes[1], w3_scales), (w2_plane, w2_scales)):
-            by_row = dram.rearrange("e s (q r) i -> r q (e s) i", r=4)
-            for r in range(4):
-                nc.gpsimd.dma_start(out=plane[r:P:32].bitcast(I32), in_=by_row[r].bitcast(I32))
+        by_row = w2_scales.rearrange("e s (q r) i -> r q (e s) i", r=4)
+        for r in range(4):
+            nc.gpsimd.dma_start(out=w2_plane[r:P:32].bitcast(I32), in_=by_row[r].bitcast(I32))
         make_identity(nc, identity[:])
 
+        tok_codes = {}
+
         def tokens(s):
+            x_bf = ring.tile([P, T, 4], BF16, name="x_bf", align_bytes=64)
+            tok_codes[s] = ring.tile([P, T], U32, name="tok_codes", align_bytes=64)
             cut = T - VECTOR_COLS[s]
-            dst, src = interleave(x_raw[s][:, :, :cut], x_bf[s][:, :cut, :])
+            dst, src = interleave(x_raw[s][:, :, :cut], x_bf[:, :cut, :])
             nc.scalar.activation(dst, src, COPY)
-            dst, src = interleave(x_raw[s][:, :, cut:], x_bf[s][:, cut:, :])
-            nc.vector.tensor_copy(dst, src)
+            if cut < T:
+                dst, src = interleave(x_raw[s][:, :, cut:], x_bf[:, cut:, :])
+                nc.vector.tensor_copy(dst, src)
             nc.vector.quantize_mx(
                 out=tok_codes[s][:].bitcast(E4M3),
                 scales=tok_scales[s][:],
-                in_=x_bf[s][:].rearrange("p w j -> p (w j)"),
+                in_=x_bf[:].rearrange("p w j -> p (w j)"),
             )
 
         def gather(s, cuts):
@@ -140,8 +151,10 @@ def tile_moe_rag_glu_relu_kernel(
                     stop=(s == PASSES - 1),
                 )
 
+        tokens(0)
         for s in range(PASSES):
-            tokens(s)
+            if s + 1 < PASSES:
+                tokens(s + 1)
             gather(s, LIST_CUTS if s < PASSES - 1 else LAST_CUTS)
             for m in range(TILES):
                 multiply(s, m)
@@ -184,14 +197,11 @@ def tile_moe_rag_glu_relu_kernel(
                     stop=True,
                 )
             nc.scalar.copy(y_slots[:, :, cols], y[:])
-            if m > 0:
-                first = 0 if m == 1 else P * m
-                for t in range(2):
-                    nc.vector.tensor_tensor(
-                        y_tokens[t][:].indirect(offsets[:, first // 16 : P * (m + 1) // 16]),
-                        y_slots[:, t, first : P * (m + 1)],
-                        gates[:, t, first : P * (m + 1)],
-                        MULT,
-                    )
+        for a, b in ((0, 256), (256, 384), (384, 512)):
+            for t in range(2):
+                cols = slice(a, b)
+                nc.vector.tensor_tensor(
+                    y_tokens[t][:].indirect(offsets[:, a // 16 : b // 16]), y_slots[:, t, cols], gates[:, t, cols], MULT
+                )
         for t in range(2):
             nc.sync.dma_start(out=out[P * t : P * (t + 1), :], in_=y_tokens[t][:])

@@ -25,9 +25,10 @@ N = 256
 PASSES = 5
 TILES = 4
 TILE_EXPERT = (0, 1, 1, 1)
-VECTOR_COLS = (256, 0, 0, 0, 128)
+CAST_CUTS = (((0, 128, 256), (256, 320, 512)),) + (((0, 512, 512),),) * 4
 LIST_CUTS = ((0, 128), (128, 512))
-LAST_CUTS = ((0, 256), (256, 512))
+LAST_CUTS = ((128, 384), (384, 512), (0, 128))
+TILE_ORDER = (1, 2, 3, 0)
 
 
 def interleave(ap_in, ap_out):
@@ -87,23 +88,24 @@ def tile_moe_rag_glu_relu_kernel(
         load_x(0, slice(0, 256))
         load_x(0, slice(256, 512))
         nc.sync.dma_start(offsets[:], offs)
-        load_x(1)
-        for plane, dram in ((planes[0], w1_scales), (planes[1], w3_scales)):
+        for w, dram in enumerate((w1_scales, w3_scales)):
             by_row = dram.rearrange("e s (q r) i -> r q (e s) i", r=4)
             for r in range(4):
-                nc.sync.dma_start(out=plane[r:P:32].bitcast(I32), in_=by_row[r].bitcast(I32))
+                nc.sync.dma_start(out=planes[w][r:P:32].bitcast(I32), in_=by_row[r].bitcast(I32))
+            if w == 0:
+                load_x(1)
         load_w(0, both)
         load_x(2)
         load_w(1, both)
         load_x(3)
-        load_w(2, both)
         load_x(4)
+        load_w(2, both)
         load_w(3, both)
         nc.sync.dma_start(
             out=w2_codes[:].bitcast(I32), in_=w2_words[:, 0].rearrange("e p b -> p e b").bitcast(I32)
         )
-        load_w(4, slice(0, 1))
         load_w(4, slice(1, 2))
+        load_w(4, slice(0, 1))
         nc.sync.dma_start(out=gates[:], in_=gate.rearrange("(t p) s -> p t s", p=P))
 
         for s in range(PASSES):
@@ -119,17 +121,18 @@ def tile_moe_rag_glu_relu_kernel(
         def tokens(s):
             x_bf = ring.tile([P, T, 4], BF16, name="x_bf", align_bytes=64)
             tok_codes[s] = ring.tile([P, T], U32, name="tok_codes", align_bytes=64)
-            cut = T - VECTOR_COLS[s]
-            dst, src = interleave(x_raw[s][:, :, :cut], x_bf[:, :cut, :])
-            nc.scalar.activation(dst, src, COPY)
-            if cut < T:
-                dst, src = interleave(x_raw[s][:, :, cut:], x_bf[:, cut:, :])
-                nc.vector.tensor_copy(dst, src)
-            nc.vector.quantize_mx(
-                out=tok_codes[s][:].bitcast(E4M3),
-                scales=tok_scales[s][:],
-                in_=x_bf[:].rearrange("p w j -> p (w j)"),
-            )
+            for a, cut, b in CAST_CUTS[s]:
+                if a < cut:
+                    dst, src = interleave(x_raw[s][:, :, a:cut], x_bf[:, a:cut, :])
+                    nc.scalar.activation(dst, src, COPY)
+                if cut < b:
+                    dst, src = interleave(x_raw[s][:, :, cut:b], x_bf[:, cut:b, :])
+                    nc.vector.tensor_copy(dst, src)
+                nc.vector.quantize_mx(
+                    out=tok_codes[s][:, a:b].bitcast(E4M3),
+                    scales=tok_scales[s][:, a:b],
+                    in_=x_bf[:, a:b, :].rearrange("p w j -> p (w j)"),
+                )
 
         def gather(s, cuts):
             for a, b in cuts:
@@ -156,48 +159,54 @@ def tile_moe_rag_glu_relu_kernel(
             if s + 1 < PASSES:
                 tokens(s + 1)
             gather(s, LIST_CUTS if s < PASSES - 1 else LAST_CUTS)
-            for m in range(TILES):
+            for m in TILE_ORDER if s == PASSES - 1 else range(TILES):
                 multiply(s, m)
 
-        for m in range(TILES):
-            e = TILE_EXPERT[m]
-            cols = slice(P * m, P * (m + 1))
-            a_pos = held.tile([P, H], F32, name=f"a_pos{m}")
-            nc.scalar.activation(a_pos[:], banks[m][0][:], RELU)
-            h = held.tile([P, 2, P, 2], BF16, name=f"h{m}", align_bytes=64)
+        h, h_in, turned, h_codes, h_scales, y, a_pos = {}, {}, {}, {}, {}, {}, {}
+        for m in TILE_ORDER:
+            a_pos[m] = held.tile([P, H], F32, name=f"a_pos{m}")
+            nc.scalar.activation(a_pos[m][:], banks[m][0][:], RELU)
+        for m in TILE_ORDER:
+            h[m] = held.tile([P, 2, P, 2], BF16, name=f"h{m}", align_bytes=64)
             nc.vector.tensor_tensor(
-                h[:],
+                h[m][:],
                 banks[m][1][:].rearrange("p (q u v) -> p u q v", u=2, v=2),
-                a_pos[:].rearrange("p (q u v) -> p u q v", u=2, v=2),
+                a_pos[m][:].rearrange("p (q u v) -> p u q v", u=2, v=2),
                 MULT,
             )
-            turned = psum.tile([P, 2, P], F32, name=f"turned{m}", tag=f"bank0_{m}")
-            pairs = h[:].rearrange("p u q v -> p (u q v)").bitcast(F32)
+        for m in TILE_ORDER:
+            turned[m] = psum.tile([P, 2, P], F32, name=f"turned{m}", tag=f"bank0_{m}")
+            pairs = h[m][:].rearrange("p u q v -> p (u q v)").bitcast(F32)
             for u in range(2):
-                nc.tensor.transpose(turned[:, u, :], pairs[:, P * u : P * (u + 1)], identity[:])
-            h_in = held.tile([P, P, 4], BF16, name=f"h_in{m}", align_bytes=64)
+                nc.tensor.transpose(turned[m][:, u, :], pairs[:, P * u : P * (u + 1)], identity[:])
+        for m in TILE_ORDER:
+            h_in[m] = held.tile([P, P, 4], BF16, name=f"h_in{m}", align_bytes=64)
             nc.scalar.copy(
-                h_in[:].rearrange("p c d -> p (c d)").bitcast(F32).rearrange("p (c u) -> p c u", u=2),
-                turned[:].rearrange("p u c -> p c u"),
+                h_in[m][:].rearrange("p c d -> p (c d)").bitcast(F32).rearrange("p (c u) -> p c u", u=2),
+                turned[m][:].rearrange("p u c -> p c u"),
             )
-            h_codes = held.tile([P, P], U32, name=f"h_codes{m}", align_bytes=64)
-            h_scales = held.tile([P, P], U8, name=f"h_scales{m}", align_bytes=64)
+        for m in TILE_ORDER:
+            h_codes[m] = held.tile([P, P], U32, name=f"h_codes{m}", align_bytes=64)
+            h_scales[m] = held.tile([P, P], U8, name=f"h_scales{m}", align_bytes=64)
             nc.vector.quantize_mx(
-                out=h_codes[:].bitcast(E4M3), scales=h_scales[:], in_=h_in[:].rearrange("p c d -> p (c d)")
+                out=h_codes[m][:].bitcast(E4M3), scales=h_scales[m][:], in_=h_in[m][:].rearrange("p c d -> p (c d)")
             )
-            y = psum.tile([P, 2, P], F32, name=f"y{m}", tag=f"bank1_{m}")
+        for m in TILE_ORDER:
+            e = TILE_EXPERT[m]
+            y[m] = psum.tile([P, 2, P], F32, name=f"y{m}", tag=f"bank1_{m}")
             for t in range(2):
                 nc.tensor.matmul_mx(
-                    out=y[:, t, :],
+                    out=y[m][:, t, :],
                     lhsT=w2_codes[:, e, 2 * P * t : 2 * P * (t + 1)].bitcast(E2M1),
                     lhsT_scale=w2_plane[:, e, P * t : P * (t + 1)],
-                    rhs=h_codes[:].bitcast(E4M3),
-                    rhs_scale=h_scales[:],
+                    rhs=h_codes[m][:].bitcast(E4M3),
+                    rhs_scale=h_scales[m][:],
                     start=True,
                     stop=True,
                 )
-            nc.scalar.copy(y_slots[:, :, cols], y[:])
-        for a, b in ((0, 256), (256, 384), (384, 512)):
+        for m in TILE_ORDER:
+            nc.scalar.copy(y_slots[:, :, P * m : P * (m + 1)], y[m][:])
+        for a, b in ((128, 384), (384, 512), (0, 128)):
             for t in range(2):
                 cols = slice(a, b)
                 nc.vector.tensor_tensor(

from contextlib import ExitStack

import concourse.mybir as mybir
from concourse.masks import make_identity

FLOPS = 2818572288

F32 = mybir.dt.float32
BF16 = mybir.dt.bfloat16
I32 = mybir.dt.int32
U32 = mybir.dt.uint32
U16 = mybir.dt.uint16
U8 = mybir.dt.uint8
E4M3 = mybir.dt.float8_e4m3fn_x4
E2M1 = mybir.dt.float4_e2m1fn_x4
COPY = mybir.ActivationFunctionType.Copy
RELU = mybir.ActivationFunctionType.Relu
MULT = mybir.AluOpType.mult

P = 128
T = 512
E = 2
H = 512
N = 256
PASSES = 5
TILES = 4
TILE_EXPERT = (0, 1, 1, 1)
CAST_CUTS = (((0, 128, 256), (256, 320, 512)),) + (((0, 512, 512),),) * 4
LIST_CUTS = ((0, 128), (128, 512))
LAST_CUTS = ((128, 384), (384, 512), (0, 128))
TILE_ORDER = (1, 2, 3, 0)


def interleave(ap_in, ap_out):
    return (
        ap_out.rearrange("p (c i) t -> p c t i", i=4),
        ap_in.rearrange("p t (c i) -> p c t i", i=4),
    )


def tile_moe_rag_glu_relu_kernel(
    tc, xT, w1_words, w1_scales, w3_words, w3_scales, w2_words, w2_scales, gate, offs, out
):
    nc = tc.nc
    with ExitStack() as ctx:
        held = ctx.enter_context(tc.tile_pool(name="held", bufs=1))
        ring = ctx.enter_context(tc.tile_pool(name="ring", bufs=2))
        psum = ctx.enter_context(tc.psum_pool(name="psum", bufs=1))

        offsets = held.tile([P, T // 16], U16, name="offsets")
        x_raw = {}
        tok_scales = [held.tile([P, T], U8, name=f"tok_scales{s}", align_bytes=64) for s in range(PASSES)]
        slot_codes = [held.tile([P, T], U32, name=f"slot_codes{s}", align_bytes=64) for s in range(PASSES)]
        slot_scales = [held.tile([P, T], U8, name=f"slot_scales{s}", align_bytes=64) for s in range(PASSES)]
        words = [
            [held.tile([P, E, 2 * H], U8, name=f"words{w}_{s}", align_bytes=64) for w in range(2)]
            for s in range(PASSES)
        ]
        planes = [held.tile([P, E * PASSES, H], U8, name=f"planes{w}", align_bytes=64) for w in range(2)]
        w2_codes = held.tile([P, E, 2 * N], U8, name="w2_codes", align_bytes=64)
        w2_plane = held.tile([P, E, N], U8, name="w2_plane", align_bytes=64)
        gates = held.tile([P, 2, T], F32, name="gates")
        identity = held.tile([P, P], F32, name="identity")
        y_slots = held.tile([P, 2, T], F32, name="y_slots")
        y_tokens = [held.tile([P, T], F32, name=f"y_tokens{t}") for t in range(2)]
        banks = [[psum.tile([P, H], F32, name=f"bank{w}_{m}", tag=f"bank{w}_{m}") for w in range(2)] for m in range(TILES)]

        w_dram = (w1_words, w3_words)

        def load_x(s, cols=slice(0, T)):
            if s not in x_raw:
                x_raw[s] = ring.tile([P, 4, T], F32, name="x_raw", bufs=3)
            nc.sync.dma_start(
                out=x_raw[s][:, :, cols],
                in_=xT[4 * P * s : 4 * P * (s + 1), cols].rearrange("(p j) w -> p j w", j=4),
            )

        def load_w(s, experts):
            for w in range(2):
                nc.sync.dma_start(
                    out=words[s][w][:, experts, :].bitcast(I32),
                    in_=w_dram[w][experts, s].rearrange("e p b -> p e b").bitcast(I32),
                )

        nc.vector.memset(planes[0][:].bitcast(I32), 0)
        nc.gpsimd.memset(planes[1][:].bitcast(I32), 0)
        both = slice(0, E)
        load_x(0, slice(0, 256))
        load_x(0, slice(256, 512))
        nc.sync.dma_start(offsets[:], offs)
        for w, dram in enumerate((w1_scales, w3_scales)):
            by_row = dram.rearrange("e s (q r) i -> r q (e s) i", r=4)
            for r in range(4):
                nc.sync.dma_start(out=planes[w][r:P:32].bitcast(I32), in_=by_row[r].bitcast(I32))
            if w == 0:
                load_x(1)
        load_w(0, both)
        load_x(2)
        load_w(1, both)
        load_x(3)
        load_x(4)
        load_w(2, both)
        load_w(3, both)
        nc.sync.dma_start(
            out=w2_codes[:].bitcast(I32), in_=w2_words[:, 0].rearrange("e p b -> p e b").bitcast(I32)
        )
        load_w(4, slice(1, 2))
        load_w(4, slice(0, 1))
        nc.sync.dma_start(out=gates[:], in_=gate.rearrange("(t p) s -> p t s", p=P))

        for s in range(PASSES):
            nc.vector.memset(tok_scales[s][:].bitcast(I32), 0)
        nc.vector.memset(w2_plane[:].bitcast(I32), 0)
        by_row = w2_scales.rearrange("e s (q r) i -> r q (e s) i", r=4)
        for r in range(4):
            nc.gpsimd.dma_start(out=w2_plane[r:P:32].bitcast(I32), in_=by_row[r].bitcast(I32))
        make_identity(nc, identity[:])

        tok_codes = {}

        def tokens(s):
            x_bf = ring.tile([P, T, 4], BF16, name="x_bf", align_bytes=64)
            tok_codes[s] = ring.tile([P, T], U32, name="tok_codes", align_bytes=64)
            for a, cut, b in CAST_CUTS[s]:
                if a < cut:
                    dst, src = interleave(x_raw[s][:, :, a:cut], x_bf[:, a:cut, :])
                    nc.scalar.activation(dst, src, COPY)
                if cut < b:
                    dst, src = interleave(x_raw[s][:, :, cut:b], x_bf[:, cut:b, :])
                    nc.vector.tensor_copy(dst, src)
                nc.vector.quantize_mx(
                    out=tok_codes[s][:, a:b].bitcast(E4M3),
                    scales=tok_scales[s][:, a:b],
                    in_=x_bf[:, a:b, :].rearrange("p w j -> p (w j)"),
                )

        def gather(s, cuts):
            for a, b in cuts:
                picked = offsets[:, a // 16 : b // 16]
                nc.vector.tensor_copy(slot_codes[s][:, a:b], tok_codes[s][:].indirect(picked))
                nc.vector.tensor_copy(slot_scales[s][:, a:b], tok_scales[s][:].indirect(picked))

        def multiply(s, m):
            e = TILE_EXPERT[m]
            cols = slice(P * m, P * (m + 1))
            for w in range(2):
                nc.tensor.matmul_mx(
                    out=banks[m][w][:],
                    lhsT=slot_codes[s][:, cols].bitcast(E4M3),
                    lhsT_scale=slot_scales[s][:, cols],
                    rhs=words[s][w][:, e, :].bitcast(E2M1),
                    rhs_scale=planes[w][:, e * PASSES + s, :],
                    start=(s == 0),
                    stop=(s == PASSES - 1),
                )

        tokens(0)
        for s in range(PASSES):
            if s + 1 < PASSES:
                tokens(s + 1)
            gather(s, LIST_CUTS if s < PASSES - 1 else LAST_CUTS)
            for m in TILE_ORDER if s == PASSES - 1 else range(TILES):
                multiply(s, m)

        h, h_in, turned, h_codes, h_scales, y, a_pos = {}, {}, {}, {}, {}, {}, {}
        for m in TILE_ORDER:
            a_pos[m] = held.tile([P, H], F32, name=f"a_pos{m}")
            nc.scalar.activation(a_pos[m][:], banks[m][0][:], RELU)
        for m in TILE_ORDER:
            h[m] = held.tile([P, 2, P, 2], BF16, name=f"h{m}", align_bytes=64)
            nc.vector.tensor_tensor(
                h[m][:],
                banks[m][1][:].rearrange("p (q u v) -> p u q v", u=2, v=2),
                a_pos[m][:].rearrange("p (q u v) -> p u q v", u=2, v=2),
                MULT,
            )
        for m in TILE_ORDER:
            turned[m] = psum.tile([P, 2, P], F32, name=f"turned{m}", tag=f"bank0_{m}")
            pairs = h[m][:].rearrange("p u q v -> p (u q v)").bitcast(F32)
            for u in range(2):
                nc.tensor.transpose(turned[m][:, u, :], pairs[:, P * u : P * (u + 1)], identity[:])
        for m in TILE_ORDER:
            h_in[m] = held.tile([P, P, 4], BF16, name=f"h_in{m}", align_bytes=64)
            nc.scalar.copy(
                h_in[m][:].rearrange("p c d -> p (c d)").bitcast(F32).rearrange("p (c u) -> p c u", u=2),
                turned[m][:].rearrange("p u c -> p c u"),
            )
        for m in TILE_ORDER:
            h_codes[m] = held.tile([P, P], U32, name=f"h_codes{m}", align_bytes=64)
            h_scales[m] = held.tile([P, P], U8, name=f"h_scales{m}", align_bytes=64)
            nc.vector.quantize_mx(
                out=h_codes[m][:].bitcast(E4M3), scales=h_scales[m][:], in_=h_in[m][:].rearrange("p c d -> p (c d)")
            )
        for m in TILE_ORDER:
            e = TILE_EXPERT[m]
            y[m] = psum.tile([P, 2, P], F32, name=f"y{m}", tag=f"bank1_{m}")
            for t in range(2):
                nc.tensor.matmul_mx(
                    out=y[m][:, t, :],
                    lhsT=w2_codes[:, e, 2 * P * t : 2 * P * (t + 1)].bitcast(E2M1),
                    lhsT_scale=w2_plane[:, e, P * t : P * (t + 1)],
                    rhs=h_codes[m][:].bitcast(E4M3),
                    rhs_scale=h_scales[m][:],
                    start=True,
                    stop=True,
                )
        for m in TILE_ORDER:
            nc.scalar.copy(y_slots[:, :, P * m : P * (m + 1)], y[m][:])
        for a, b in ((128, 384), (384, 512), (0, 128)):
            for t in range(2):
                cols = slice(a, b)
                nc.vector.tensor_tensor(
                    y_tokens[t][:].indirect(offsets[:, a // 16 : b // 16]), y_slots[:, t, cols], gates[:, t, cols], MULT
                )
        for t in range(2):
            nc.sync.dma_start(out=out[P * t : P * (t + 1), :], in_=y_tokens[t][:])
